import numpy as np
import ml_dtypes


def mxq(x, axis, fmt="e4m3"):
    dtype, down = {"e4m3": (ml_dtypes.float8_e4m3fn, 7), "e5m2": (ml_dtypes.float8_e5m2, 14)}[fmt]
    v = np.moveaxis(np.asarray(x, np.float32).astype(ml_dtypes.bfloat16).astype(np.float64), axis, -1)
    blocks = v.reshape(v.shape[:-1] + (-1, 32))
    amax = np.abs(blocks).max(-1, keepdims=True)
    byte = np.maximum(np.where(amax > 0, np.frexp(amax)[1] - 1 + 127, 0) - down, 1)
    scale = np.exp2(byte - 127.0)
    codes = (blocks / scale).astype(np.float32).astype(dtype).astype(np.float64)
    return np.moveaxis((codes * scale).reshape(v.shape), -1, axis)


WIDE = False


def mx_kscale(k):
    if not WIDE:
        return np.ones(k)
    levels = np.array([10, -10, 5, -5, 0])
    if k % 512:
        return np.exp2(np.random.permutation(np.resize(levels, k // 32))).repeat(32)
    a = np.empty((k // 512, 16))
    for p in range(k // 512):
        a[p, :8] = np.random.permutation(np.resize(levels, 8))
        for g in range(8):
            far = levels[np.abs(levels - a[p, g]) >= 10]
            a[p, g + 8] = far[np.random.randint(len(far))]
    return np.exp2(a.ravel()).repeat(32)


def f64(x):
    return np.asarray(x).astype(np.float64)


def striped(idx):
    return np.tile(np.asarray(idx).reshape(-1, 16).T, (8, 1)).astype(np.uint16)


def unstriped(offs):
    return offs[:16].T.reshape(-1).astype(np.int64)


E2M1 = np.array([0.0, 0.5, 1.0, 1.5, 2.0, 3.0, 4.0, 6.0, -0.0, -0.5, -1.0, -1.5, -2.0, -3.0, -4.0, -6.0])


def pack_weight(w, fmt):
    k, n = w.shape
    w = f64(np.asarray(w, np.float32).astype(ml_dtypes.bfloat16)).reshape(k // 32, 32, n)
    amax = np.abs(w).max(1)
    if fmt == "e4m3":
        byte = np.frexp(amax)[1] - 1 + 127 - 7
    else:
        mant, ex = np.frexp(amax / 6.0)
        byte = np.where(mant > 0.5, ex, ex - 1) + 127
    byte = np.clip(np.where(amax > 0, byte, 1), 1, 254)
    scaled = (w * np.exp2(127.0 - byte)[:, None, :]).reshape(k, n).astype(np.float32)
    by_word = np.ascontiguousarray(scaled.reshape(k // 512, 128, 4, n).transpose(0, 1, 3, 2))
    if fmt == "e4m3":
        words = by_word.astype(ml_dtypes.float8_e4m3fn).view(np.uint8)
    else:
        c = by_word.astype(ml_dtypes.float4_e2m1fn).view(np.uint8) & 0xF
        words = (c[..., 0::2] | (c[..., 1::2] << 4)).reshape(k // 512, 128, 2 * n)
    return np.ascontiguousarray(words), np.ascontiguousarray(byte.astype(np.uint8).reshape(k // 512, 16, n))


def unpack_weight(words, scales, fmt):
    g, _, n = scales.shape
    words = np.ascontiguousarray(words).reshape(g, 128, n, -1)
    if fmt == "e4m3":
        vals = words.view(ml_dtypes.float8_e4m3fn).astype(np.float64)
    else:
        nib = np.empty((g, 128, n, 4), np.uint8)
        nib[..., 0::2] = words & 0xF
        nib[..., 1::2] = words >> 4
        vals = E2M1[nib]
    vals = vals * np.repeat(np.exp2(scales.astype(np.float64) - 127.0), 8, axis=1)[..., None]
    return vals.transpose(0, 1, 3, 2).reshape(g * 512, n)


def sigmoid(v):
    return 1.0 / (1.0 + np.exp(-v))


D, E, T, I, Q, G, U = 512, 512, 2048, 512, 128, 64, 256


def setup_inputs():
    n = np.random.standard_normal
    idx2 = np.random.permutation(U)[:G]
    idx = np.random.permutation(T)[:I]
    fd = mx_kscale(D)
    fe = mx_kscale(E)
    keysp = pack_weight(n((D, T)) / fd[:, None], "e4m3")
    valsp = pack_weight(n((E, T)) / fe[:, None], "e4m3")
    return {
        "query": (n((D, Q)) * 0.7 / np.sqrt(D) * fd[:, None]).astype(np.float32),
        "pquery": (n((D, Q)) * 1.0 / np.sqrt(D) * fd[:, None]).astype(np.float32),
        "keys_words": keysp[0],
        "keys_scales": keysp[1],
        "pgsum": (n((D, U)) / fd[:, None]).astype(np.float32),
        "reserve": (np.random.uniform(20.0, 100.0, (Q, 1))).astype(np.float32),
        "gout": (n((E, Q)) * 1 / np.sqrt(E) * fe[:, None]).astype(np.float32),
        "vals_words": valsp[0],
        "vals_scales": valsp[1],
        "base": (0.5 * n((Q, I))).astype(np.float32),
        "offs2": striped(idx2),
        "offs": striped(idx),
    }


def reference(query, pquery, keys_words, keys_scales, pgsum, reserve, gout, vals_words, vals_scales, base, offs2, offs):
    idx2 = unstriped(offs2)
    idx = unstriped(offs)
    keysu = unpack_weight(keys_words, keys_scales, "e4m3")
    valsu = unpack_weight(vals_words, vals_scales, "e4m3")
    pqueryq = mxq(f64(pquery), 0, "e4m3")
    pgsumidx2q = mxq(f64(pgsum)[:, idx2], 0, "e4m3")
    h0 = pqueryq.T @ pgsumidx2q
    g1 = sigmoid(h0)
    gr = np.repeat(g1, I // G, axis=1)
    queryq = mxq(f64(query), 0, "e4m3")
    keysidxg = keysu[:, idx]
    a = queryq.T @ keysidxg
    p = np.exp(a) * gr
    z = np.sum(p, axis=1, keepdims=True) + f64(reserve)
    goutq = mxq(f64(gout), 0, "e4m3")
    valsidxg = valsu[:, idx]
    c0 = goutq.T @ valsidxg
    dz = np.sum(c0 * p / np.square(z) * (-1.0), axis=1, keepdims=True)
    dp = c0 / z + dz
    da = dp * gr * np.exp(a)
    hda = da * 512.0 * 2.0 * 512.0
    hdp = hda * np.exp(a) * gr
    hdz = np.sum(hdp, axis=1, keepdims=True)
    hz = np.sum(hdp * c0 / np.square(z) * (-1.0), axis=1, keepdims=True) + np.sum(hdz * (-1.0) * c0 * p / np.square(np.square(z)) * (-1.0), axis=1, keepdims=True) * z * 2.0
    hp = hdz * (-1.0) / np.square(z) * c0 + hz
    ha = hda * dp * gr * np.exp(a) + hp * gr * np.exp(a)
    y = ha + f64(base)
    return y

@@ -1,0 +1,178 @@
+import math
+from contextlib import ExitStack
+
+import concourse.mybir as mybir
+
+F32 = mybir.dt.float32
+BF16 = mybir.dt.bfloat16
+I32 = mybir.dt.int32
+U32 = mybir.dt.uint32
+U16 = mybir.dt.uint16
+U8 = mybir.dt.uint8
+FP8X4 = mybir.dt.float8_e4m3fn_x4
+ACT = mybir.ActivationFunctionType
+ALU = mybir.AluOpType
+
+P = 128
+PACK = 4
+POOL = 2048
+SLOTS = 512
+ROWS = 128
+PAGES = 64
+TABLE = 256
+PER_PAGE = SLOTS // PAGES
+HALF = SLOTS // 2
+VALS_PLANE = 4
+PENALTY = 512.0 * 2.0 * 512.0
+ROOT = math.sqrt(PENALTY)
+
+FLOPS = 2 * 512 * ROWS * (SLOTS + SLOTS + PAGES)
+
+
+def tile_attend_gppagetablegate_kernel(tc, query, pquery, keys_words, keys_scales, pgsum, reserve, gout,
+                                        vals_words, vals_scales, base, offs2, offs, out):
+    nc = tc.nc
+    with ExitStack() as ctx:
+        sb = ctx.enter_context(tc.tile_pool(name="sb", bufs=1))
+        ps = ctx.enter_context(tc.psum_pool(name="ps", bufs=1))
+
+        def load_words(name, words, tag):
+            pool = sb.tile([P, POOL], U32, name=name, tag=tag, align_bytes=64)
+            nc.sync.dma_start(out=pool[:].bitcast(I32), in_=words[0].rearrange("p n t -> p (n t)").bitcast(I32))
+            return pool
+
+        def load_scales(queue, pool, scales, first):
+            for quad in range(4):
+                rows = pool[32 * quad + first : 32 * quad + first + 4, :]
+                queue.dma_start(out=rows.bitcast(I32), in_=scales[0, 4 * quad : 4 * quad + 4, :].bitcast(I32))
+
+        def load_rows(name, src, width, tag):
+            raw = sb.tile([P, PACK, width], F32, name=name, tag=tag, align_bytes=64)
+            nc.sync.dma_start(out=raw[:], in_=src.rearrange("(p j) w -> p j w", j=PACK))
+            return raw
+
+        def interleave(name, raw):
+            grouped = sb.tile([P, ROWS, PACK], BF16, name=name, tag=name, align_bytes=64)
+            nc.scalar.activation(out=grouped[:].rearrange("p (c i) t -> p c t i", i=4),
+                                 in_=raw[:].rearrange("p t (c i) -> p c t i", i=4), func=ACT.Copy)
+            return grouped
+
+        def quantize(name, grouped, width, tag):
+            codes = sb.tile([P, width], U32, name=name + "_codes", tag=tag, align_bytes=64)
+            scales = sb.tile([P, width], U8, name=name + "_scales", align_bytes=64)
+            nc.vector.quantize_mx(out=codes[:].bitcast(FP8X4), scales=scales[:],
+                                  in_=grouped[:].rearrange("p w j -> p (w j)"))
+            return codes, scales
+
+        key_scale_pool = sb.tile([P, POOL], U8, tag="key_scale_pool", align_bytes=64)
+        nc.vector.memset(key_scale_pool[:].bitcast(I32), 0)
+
+        reserve_sb = sb.tile([ROWS, 1], F32, tag="key_pool", align_bytes=64)
+        nc.sync.dma_start(out=reserve_sb[:], in_=reserve)
+        page_list = sb.tile([P, PAGES // 16], U16)
+        nc.sync.dma_start(page_list[:], offs2)
+        slot_list = sb.tile([P, SLOTS // 16], U16)
+        nc.sync.dma_start(slot_list[:], offs)
+        pgsum_raw = load_rows("pgsum_raw", pgsum, TABLE, "pgsum_raw")
+        pquery_raw = load_rows("pquery_raw", pquery, ROWS, "pquery_raw")
+        query_raw = load_rows("query_raw", query, ROWS, "query_raw")
+        load_scales(nc.sync, key_scale_pool, keys_scales, 0)
+        twice_reserve = sb.tile([ROWS, 1], F32)
+        nc.vector.tensor_scalar_mul(twice_reserve[:], reserve_sb[:], 2.0)
+        key_pool = load_words("key_pool", keys_words, "key_pool")
+
+        pages_bf = sb.tile([P, PAGES, PACK], BF16, align_bytes=64)
+        for j in range(PACK):
+            nc.vector.tensor_copy(pages_bf[:, :, j], pgsum_raw[:, j, :].indirect(page_list[:]))
+        pquery_bf = interleave("pquery_bf", pquery_raw)
+        query_bf = interleave("query_bf", query_raw)
+        val_scale_pool = sb.tile([P, POOL], U8, tag="pquery_raw", align_bytes=64)
+        nc.vector.memset(val_scale_pool[:].bitcast(I32), 0)
+        load_scales(nc.sync, val_scale_pool, vals_scales, VALS_PLANE)
+        pquery_codes, pquery_scales = quantize("pquery", pquery_bf, ROWS, "pquery_codes")
+        gout_raw = load_rows("gout_raw", gout, ROWS, "pquery_bf")
+        page_codes, page_scales = quantize("page", pages_bf, PAGES, "page_codes")
+        query_codes, query_scales = quantize("query", query_bf, ROWS, "query_codes")
+        val_pool = load_words("val_pool", vals_words, "query_bf")
+        page_score = ps.tile([ROWS, PAGES], F32)
+        nc.tensor.matmul_mx(out=page_score[:], lhsT=pquery_codes[:].bitcast(FP8X4), lhsT_scale=pquery_scales[:],
+                            rhs=page_codes[:].bitcast(FP8X4), rhs_scale=page_scales[:], start=True, stop=True)
+        half_tanh = sb.tile([ROWS, PAGES], F32)
+        nc.scalar.activation(out=half_tanh[:], in_=page_score[:], func=ACT.Tanh, scale=0.5)
+
+        key_scales = sb.tile([P, SLOTS], U8, align_bytes=64)
+        nc.vector.tensor_copy(key_scales[:], key_scale_pool[:].indirect(slot_list[:]))
+        base_sb = sb.tile([ROWS, SLOTS], F32, tag="key_scale_pool", align_bytes=64)
+        nc.sync.dma_start(out=base_sb[:], in_=base)
+        key_words = sb.tile([P, SLOTS], U32, tag="key_words", align_bytes=64)
+        nc.vector.tensor_copy(key_words[:], key_pool[:].indirect(slot_list[:]))
+        score = ps.tile([ROWS, SLOTS], F32)
+        nc.tensor.matmul_mx(out=score[:], lhsT=query_codes[:].bitcast(FP8X4), lhsT_scale=query_scales[:],
+                            rhs=key_words[:].bitcast(FP8X4), rhs_scale=key_scales[:], start=True, stop=True)
+        gout_bf = interleave("gout_bf", gout_raw)
+        exp_score = sb.tile([ROWS, SLOTS], F32, tag="pquery_bf", align_bytes=64)
+        nc.scalar.activation(out=exp_score[:], in_=score[:], func=ACT.Exp)
+
+        val_scales = sb.tile([P, SLOTS], U8, tag="key_pool", align_bytes=64)
+        nc.vector.tensor_copy(val_scales[:], val_scale_pool[:].indirect(slot_list[:]))
+        gout_codes, gout_scales = quantize("gout", gout_bf, ROWS, "key_words")
+
+        gated = sb.tile([ROWS, SLOTS], F32, tag="pquery_raw", align_bytes=64)
+        gated_sum = sb.tile([ROWS, 1], F32, tag="gout_bf", align_bytes=64)
+        nc.vector.scalar_tensor_tensor(
+            out=gated[:].rearrange("q (g i) -> q g i", i=PER_PAGE),
+            in0=half_tanh[:].unsqueeze(2).to_broadcast([ROWS, PAGES, PER_PAGE]), scalar=1.0,
+            in1=exp_score[:].rearrange("q (g i) -> q g i", i=PER_PAGE),
+            op0=ALU.add, op1=ALU.mult, accum_out=gated_sum[:])
+        total = sb.tile([ROWS, 1], F32)
+        nc.scalar.activation(out=total[:], in_=gated_sum[:], func=ACT.Identity, bias=twice_reserve[:])
+
+        val_words = sb.tile([P, SLOTS], U32, tag="pquery_bf", align_bytes=64)
+        dread = ps.tile([ROWS, SLOTS], F32)
+        for h in range(2):
+            cols = slice(h * HALF, (h + 1) * HALF)
+            nc.vector.tensor_copy(val_words[:, cols],
+                                  val_pool[:].indirect(slot_list[:, h * HALF // 16 : (h + 1) * HALF // 16]))
+            nc.tensor.matmul_mx(out=dread[:, cols], lhsT=gout_codes[:].bitcast(FP8X4), lhsT_scale=gout_scales[:],
+                                rhs=val_words[:, cols].bitcast(FP8X4), rhs_scale=val_scales[VALS_PLANE:P, cols],
+                                start=True, stop=True)
+        inv_total = sb.tile([ROWS, 1], F32, tag="query_bf", align_bytes=64)
+        nc.vector.reciprocal(inv_total[:], total[:])
+        weight = sb.tile([ROWS, SLOTS], F32)
+        nc.scalar.activation(out=weight[:], in_=gated[:], func=ACT.Copy, scale=inv_total[:])
+        weight_sq = sb.tile([ROWS, SLOTS], F32)
+        nc.scalar.activation(out=weight_sq[:], in_=weight[:], func=ACT.Square, scale=math.sqrt(ROOT / 2.0))
+
+        scratch_v = sb.tile([ROWS, SLOTS], F32)
+        mean = sb.tile([ROWS, 1], F32)
+        nc.vector.scalar_tensor_tensor(out=scratch_v[:], in0=dread[:], scalar=inv_total[:], in1=gated[:],
+                                       op0=ALU.mult, op1=ALU.mult, accum_out=mean[:])
+        dscore = sb.tile([ROWS, SLOTS], F32)
+        nc.vector.scalar_tensor_tensor(out=dscore[:], in0=dread[:], scalar=mean[:], in1=weight[:],
+                                       op0=ALU.subtract, op1=ALU.mult)
+        shift = sb.tile([ROWS, 1], F32)
+        nc.vector.scalar_tensor_tensor(out=scratch_v[:], in0=dread[:], scalar=mean[:], in1=weight_sq[:],
+                                       op0=ALU.subtract, op1=ALU.mult, accum_out=shift[:])
+        scratch_s = sb.tile([ROWS, SLOTS], F32)
+        energy = sb.tile([ROWS, 1], F32)
+        nc.scalar.activation(out=scratch_s[:], in_=dscore[:], func=ACT.Square, scale=ROOT, accum_out=energy[:])
+        shift_sq = sb.tile([ROWS, 1], F32)
+        nc.scalar.activation(out=shift_sq[:], in_=shift[:], func=ACT.Square)
+
+        squares = []
+        rests = []
+        for h in range(2):
+            cols = slice(h * HALF, (h + 1) * HALF)
+            square = sb.tile([ROWS, HALF], F32, name="square%d" % h)
+            nc.scalar.activation(out=square[:], in_=dscore[:, cols], func=ACT.Square, scale=-ROOT, bias=shift[:])
+            rest = sb.tile([ROWS, HALF], F32, name="rest%d" % h)
+            nc.vector.scalar_tensor_tensor(out=rest[:], in0=weight[:, cols], scalar=energy[:], in1=base_sb[:, cols],
+                                           op0=ALU.mult, op1=ALU.subtract)
+            squares.append(square)
+            rests.append(rest)
+        for h in range(2):
+            cols = slice(h * HALF, (h + 1) * HALF)
+            result = sb.tile([ROWS, HALF], F32, name="result%d" % h)
+            nc.vector.scalar_tensor_tensor(out=result[:], in0=squares[h][:], scalar=shift_sq[:], in1=rests[h][:],
+                                           op0=ALU.subtract, op1=ALU.subtract)
+            nc.sync.dma_start(out=out[:, cols], in_=result[:])

@@ -41,18 +41,18 @@ def tile_attend_gppagetablegate_kernel(tc, query, pquery, keys_words, keys_scale
             nc.sync.dma_start(out=pool[:].bitcast(I32), in_=words[0].rearrange("p n t -> p (n t)").bitcast(I32))
             return pool
 
-        def load_scales(queue, pool, scales, first):
+        def load_scales(queues, pool, scales, first):
             for quad in range(4):
                 rows = pool[32 * quad + first : 32 * quad + first + 4, :]
-                queue.dma_start(out=rows.bitcast(I32), in_=scales[0, 4 * quad : 4 * quad + 4, :].bitcast(I32))
+                queues[quad].dma_start(out=rows.bitcast(I32), in_=scales[0, 4 * quad : 4 * quad + 4, :].bitcast(I32))
 
         def load_rows(name, src, width, tag):
             raw = sb.tile([P, PACK, width], F32, name=name, tag=tag, align_bytes=64)
             nc.sync.dma_start(out=raw[:], in_=src.rearrange("(p j) w -> p j w", j=PACK))
             return raw
 
-        def interleave(name, raw):
-            grouped = sb.tile([P, ROWS, PACK], BF16, name=name, tag=name, align_bytes=64)
+        def interleave(name, raw, tag):
+            grouped = sb.tile([P, ROWS, PACK], BF16, name=name, tag=tag, align_bytes=64)
             nc.scalar.activation(out=grouped[:].rearrange("p (c i) t -> p c t i", i=4),
                                  in_=raw[:].rearrange("p t (c i) -> p c t i", i=4), func=ACT.Copy)
             return grouped
@@ -66,9 +66,9 @@ def tile_attend_gppagetablegate_kernel(tc, query, pquery, keys_words, keys_scale
 
         key_scale_pool = sb.tile([P, POOL], U8, tag="key_scale_pool", align_bytes=64)
         nc.vector.memset(key_scale_pool[:].bitcast(I32), 0)
+        val_scale_pool = sb.tile([P, POOL], U8, tag="val_scale_pool", align_bytes=64)
+        nc.vector.memset(val_scale_pool[:].bitcast(I32), 0)
 
-        reserve_sb = sb.tile([ROWS, 1], F32, tag="key_pool", align_bytes=64)
-        nc.sync.dma_start(out=reserve_sb[:], in_=reserve)
         page_list = sb.tile([P, PAGES // 16], U16)
         nc.sync.dma_start(page_list[:], offs2)
         slot_list = sb.tile([P, SLOTS // 16], U16)
@@ -76,58 +76,56 @@ def tile_attend_gppagetablegate_kernel(tc, query, pquery, keys_words, keys_scale
         pgsum_raw = load_rows("pgsum_raw", pgsum, TABLE, "pgsum_raw")
         pquery_raw = load_rows("pquery_raw", pquery, ROWS, "pquery_raw")
         query_raw = load_rows("query_raw", query, ROWS, "query_raw")
-        load_scales(nc.sync, key_scale_pool, keys_scales, 0)
-        twice_reserve = sb.tile([ROWS, 1], F32)
-        nc.vector.tensor_scalar_mul(twice_reserve[:], reserve_sb[:], 2.0)
         key_pool = load_words("key_pool", keys_words, "key_pool")
+        val_pool = load_words("val_pool", vals_words, "val_pool")
+        load_scales([nc.gpsimd, nc.scalar, nc.scalar, nc.scalar], key_scale_pool, keys_scales, 0)
+        load_scales([nc.gpsimd] * 4, val_scale_pool, vals_scales, VALS_PLANE)
+        reserve_sb = sb.tile([ROWS, 1], F32)
+        nc.gpsimd.dma_start(out=reserve_sb[:], in_=reserve)
 
         pages_bf = sb.tile([P, PAGES, PACK], BF16, align_bytes=64)
         for j in range(PACK):
             nc.vector.tensor_copy(pages_bf[:, :, j], pgsum_raw[:, j, :].indirect(page_list[:]))
-        pquery_bf = interleave("pquery_bf", pquery_raw)
-        query_bf = interleave("query_bf", query_raw)
-        val_scale_pool = sb.tile([P, POOL], U8, tag="pquery_raw", align_bytes=64)
-        nc.vector.memset(val_scale_pool[:].bitcast(I32), 0)
-        load_scales(nc.sync, val_scale_pool, vals_scales, VALS_PLANE)
+        pquery_bf = interleave("pquery_bf", pquery_raw, "pquery_bf")
+        gout_raw = load_rows("gout_raw", gout, ROWS, "pquery_raw")
+        query_bf = interleave("query_bf", query_raw, "query_bf")
+        base_sb = sb.tile([ROWS, SLOTS], F32, tag="query_raw", align_bytes=64)
+        nc.sync.dma_start(out=base_sb[:], in_=base)
+        key_scales = sb.tile([P, SLOTS], U8, align_bytes=64)
+        nc.vector.tensor_copy(key_scales[:], key_scale_pool[:].indirect(slot_list[:]))
         pquery_codes, pquery_scales = quantize("pquery", pquery_bf, ROWS, "pquery_codes")
-        gout_raw = load_rows("gout_raw", gout, ROWS, "pquery_bf")
         page_codes, page_scales = quantize("page", pages_bf, PAGES, "page_codes")
         query_codes, query_scales = quantize("query", query_bf, ROWS, "query_codes")
-        val_pool = load_words("val_pool", vals_words, "query_bf")
         page_score = ps.tile([ROWS, PAGES], F32)
         nc.tensor.matmul_mx(out=page_score[:], lhsT=pquery_codes[:].bitcast(FP8X4), lhsT_scale=pquery_scales[:],
                             rhs=page_codes[:].bitcast(FP8X4), rhs_scale=page_scales[:], start=True, stop=True)
-        half_tanh = sb.tile([ROWS, PAGES], F32)
+        half_tanh = sb.tile([ROWS, PAGES], F32, tag="half_tanh", align_bytes=64)
         nc.scalar.activation(out=half_tanh[:], in_=page_score[:], func=ACT.Tanh, scale=0.5)
 
-        key_scales = sb.tile([P, SLOTS], U8, align_bytes=64)
-        nc.vector.tensor_copy(key_scales[:], key_scale_pool[:].indirect(slot_list[:]))
-        base_sb = sb.tile([ROWS, SLOTS], F32, tag="key_scale_pool", align_bytes=64)
-        nc.sync.dma_start(out=base_sb[:], in_=base)
         key_words = sb.tile([P, SLOTS], U32, tag="key_words", align_bytes=64)
         nc.vector.tensor_copy(key_words[:], key_pool[:].indirect(slot_list[:]))
         score = ps.tile([ROWS, SLOTS], F32)
         nc.tensor.matmul_mx(out=score[:], lhsT=query_codes[:].bitcast(FP8X4), lhsT_scale=query_scales[:],
                             rhs=key_words[:].bitcast(FP8X4), rhs_scale=key_scales[:], start=True, stop=True)
-        gout_bf = interleave("gout_bf", gout_raw)
-        exp_score = sb.tile([ROWS, SLOTS], F32, tag="pquery_bf", align_bytes=64)
+        exp_score = sb.tile([ROWS, SLOTS], F32)
         nc.scalar.activation(out=exp_score[:], in_=score[:], func=ACT.Exp)
+        gout_bf = interleave("gout_bf", gout_raw, "key_words")
 
         val_scales = sb.tile([P, SLOTS], U8, tag="key_pool", align_bytes=64)
         nc.vector.tensor_copy(val_scales[:], val_scale_pool[:].indirect(slot_list[:]))
-        gout_codes, gout_scales = quantize("gout", gout_bf, ROWS, "key_words")
 
-        gated = sb.tile([ROWS, SLOTS], F32, tag="pquery_raw", align_bytes=64)
-        gated_sum = sb.tile([ROWS, 1], F32, tag="gout_bf", align_bytes=64)
+        gated = sb.tile([ROWS, SLOTS], F32, tag="val_scale_pool", align_bytes=64)
+        gated_sum = sb.tile([ROWS, 1], F32)
         nc.vector.scalar_tensor_tensor(
             out=gated[:].rearrange("q (g i) -> q g i", i=PER_PAGE),
             in0=half_tanh[:].unsqueeze(2).to_broadcast([ROWS, PAGES, PER_PAGE]), scalar=1.0,
             in1=exp_score[:].rearrange("q (g i) -> q g i", i=PER_PAGE),
             op0=ALU.add, op1=ALU.mult, accum_out=gated_sum[:])
-        total = sb.tile([ROWS, 1], F32)
-        nc.scalar.activation(out=total[:], in_=gated_sum[:], func=ACT.Identity, bias=twice_reserve[:])
+        gout_codes, gout_scales = quantize("gout", gout_bf, ROWS, "half_tanh")
+        total = sb.tile([ROWS, 1], F32, tag="pquery_raw", align_bytes=64)
+        nc.scalar.activation(out=total[:], in_=reserve_sb[:], func=ACT.Identity, scale=2.0, bias=gated_sum[:])
 
-        val_words = sb.tile([P, SLOTS], U32, tag="pquery_bf", align_bytes=64)
+        val_words = sb.tile([P, SLOTS], U32, tag="key_words", align_bytes=64)
         dread = ps.tile([ROWS, SLOTS], F32)
         for h in range(2):
             cols = slice(h * HALF, (h + 1) * HALF)
@@ -136,7 +134,7 @@ def tile_attend_gppagetablegate_kernel(tc, query, pquery, keys_words, keys_scale
             nc.tensor.matmul_mx(out=dread[:, cols], lhsT=gout_codes[:].bitcast(FP8X4), lhsT_scale=gout_scales[:],
                                 rhs=val_words[:, cols].bitcast(FP8X4), rhs_scale=val_scales[VALS_PLANE:P, cols],
                                 start=True, stop=True)
-        inv_total = sb.tile([ROWS, 1], F32, tag="query_bf", align_bytes=64)
+        inv_total = sb.tile([ROWS, 1], F32, tag="val_pool", align_bytes=64)
         nc.vector.reciprocal(inv_total[:], total[:])
         weight = sb.tile([ROWS, SLOTS], F32)
         nc.scalar.activation(out=weight[:], in_=gated[:], func=ACT.Copy, scale=inv_total[:])

@@ -34,28 +34,24 @@ def tile_attend_gppagetablegate_kernel(tc, query, pquery, keys_words, keys_scale
     nc = tc.nc
     with ExitStack() as ctx:
         sb = ctx.enter_context(tc.tile_pool(name="sb", bufs=1))
+        turns = ctx.enter_context(tc.tile_pool(name="turns", bufs=1))
         ps = ctx.enter_context(tc.psum_pool(name="ps", bufs=1))
 
-        def load_words(name, words, tag):
-            pool = sb.tile([P, POOL], U32, name=name, tag=tag, align_bytes=64)
+        def load_words(pool, words):
             nc.sync.dma_start(out=pool[:].bitcast(I32), in_=words[0].rearrange("p n t -> p (n t)").bitcast(I32))
-            return pool
 
-        def load_scales(queues, pool, scales, first):
-            for quad in range(4):
-                rows = pool[32 * quad + first : 32 * quad + first + 4, :]
-                queues[quad].dma_start(out=rows.bitcast(I32), in_=scales[0, 4 * quad : 4 * quad + 4, :].bitcast(I32))
+        def load_scales(pool, scales, first):
+            for j in range(4):
+                nc.sync.dma_start(out=pool[first + j : P : 32, :].bitcast(I32), in_=scales[0, j:16:4, :].bitcast(I32))
 
         def load_rows(name, src, width, tag):
             raw = sb.tile([P, PACK, width], F32, name=name, tag=tag, align_bytes=64)
             nc.sync.dma_start(out=raw[:], in_=src.rearrange("(p j) w -> p j w", j=PACK))
             return raw
 
-        def interleave(name, raw, tag):
-            grouped = sb.tile([P, ROWS, PACK], BF16, name=name, tag=tag, align_bytes=64)
+        def interleave(grouped, raw):
             nc.scalar.activation(out=grouped[:].rearrange("p (c i) t -> p c t i", i=4),
                                  in_=raw[:].rearrange("p t (c i) -> p c t i", i=4), func=ACT.Copy)
-            return grouped
 
         def quantize(name, grouped, width, tag):
             codes = sb.tile([P, width], U32, name=name + "_codes", tag=tag, align_bytes=64)
@@ -66,9 +62,9 @@ def tile_attend_gppagetablegate_kernel(tc, query, pquery, keys_words, keys_scale
 
         key_scale_pool = sb.tile([P, POOL], U8, tag="key_scale_pool", align_bytes=64)
         nc.vector.memset(key_scale_pool[:].bitcast(I32), 0)
-        val_scale_pool = sb.tile([P, POOL], U8, tag="val_scale_pool", align_bytes=64)
-        nc.vector.memset(val_scale_pool[:].bitcast(I32), 0)
 
+        reserve_sb = turns.tile([ROWS, 16], F32, offset=4 * POOL - 32)
+        nc.sync.dma_start(out=reserve_sb[:, 0:1], in_=reserve)
         page_list = sb.tile([P, PAGES // 16], U16)
         nc.sync.dma_start(page_list[:], offs2)
         slot_list = sb.tile([P, SLOTS // 16], U16)
@@ -76,30 +72,36 @@ def tile_attend_gppagetablegate_kernel(tc, query, pquery, keys_words, keys_scale
         pgsum_raw = load_rows("pgsum_raw", pgsum, TABLE, "pgsum_raw")
         pquery_raw = load_rows("pquery_raw", pquery, ROWS, "pquery_raw")
         query_raw = load_rows("query_raw", query, ROWS, "query_raw")
-        key_pool = load_words("key_pool", keys_words, "key_pool")
-        val_pool = load_words("val_pool", vals_words, "val_pool")
-        load_scales([nc.gpsimd, nc.scalar, nc.scalar, nc.scalar], key_scale_pool, keys_scales, 0)
-        load_scales([nc.gpsimd] * 4, val_scale_pool, vals_scales, VALS_PLANE)
-        reserve_sb = sb.tile([ROWS, 1], F32)
-        nc.gpsimd.dma_start(out=reserve_sb[:], in_=reserve)
+        load_scales(key_scale_pool, keys_scales, 0)
+        twice_reserve = sb.tile([ROWS, 1], F32)
+        nc.vector.tensor_scalar_mul(twice_reserve[:], reserve_sb[:, 0:1], 2.0)
+        key_pool = turns.tile([P, POOL], U32, offset=0, align_bytes=64)
+        load_words(key_pool, keys_words)
+        val_scale_pool = turns.tile([P, POOL], U8, offset=4 * POOL, align_bytes=64)
+        nc.vector.memset(val_scale_pool[:].bitcast(I32), 0)
+        load_scales(val_scale_pool, vals_scales, VALS_PLANE)
 
         pages_bf = sb.tile([P, PAGES, PACK], BF16, align_bytes=64)
         for j in range(PACK):
             nc.vector.tensor_copy(pages_bf[:, :, j], pgsum_raw[:, j, :].indirect(page_list[:]))
-        pquery_bf = interleave("pquery_bf", pquery_raw, "pquery_bf")
+        pquery_bf = sb.tile([P, ROWS, PACK], BF16, align_bytes=64)
+        interleave(pquery_bf, pquery_raw)
         gout_raw = load_rows("gout_raw", gout, ROWS, "pquery_raw")
-        query_bf = interleave("query_bf", query_raw, "query_bf")
-        base_sb = sb.tile([ROWS, SLOTS], F32, tag="query_raw", align_bytes=64)
-        nc.sync.dma_start(out=base_sb[:], in_=base)
+        query_bf = sb.tile([P, ROWS, PACK], BF16, tag="query_bf", align_bytes=64)
+        interleave(query_bf, query_raw)
+        val_pool = sb.tile([P, POOL], U32, tag="query_raw", align_bytes=64)
+        load_words(val_pool, vals_words)
         key_scales = sb.tile([P, SLOTS], U8, align_bytes=64)
         nc.vector.tensor_copy(key_scales[:], key_scale_pool[:].indirect(slot_list[:]))
         pquery_codes, pquery_scales = quantize("pquery", pquery_bf, ROWS, "pquery_codes")
         page_codes, page_scales = quantize("page", pages_bf, PAGES, "page_codes")
-        query_codes, query_scales = quantize("query", query_bf, ROWS, "query_codes")
+        query_codes, query_scales = quantize("query", query_bf, ROWS, "key_scale_pool")
+        base_sb = sb.tile([ROWS, SLOTS], F32, tag="query_bf", align_bytes=64)
+        nc.sync.dma_start(out=base_sb[:], in_=base)
         page_score = ps.tile([ROWS, PAGES], F32)
         nc.tensor.matmul_mx(out=page_score[:], lhsT=pquery_codes[:].bitcast(FP8X4), lhsT_scale=pquery_scales[:],
                             rhs=page_codes[:].bitcast(FP8X4), rhs_scale=page_scales[:], start=True, stop=True)
-        half_tanh = sb.tile([ROWS, PAGES], F32, tag="half_tanh", align_bytes=64)
+        half_tanh = sb.tile([ROWS, PAGES], F32)
         nc.scalar.activation(out=half_tanh[:], in_=page_score[:], func=ACT.Tanh, scale=0.5)
 
         key_words = sb.tile([P, SLOTS], U32, tag="key_words", align_bytes=64)
@@ -109,32 +111,34 @@ def tile_attend_gppagetablegate_kernel(tc, query, pquery, keys_words, keys_scale
                             rhs=key_words[:].bitcast(FP8X4), rhs_scale=key_scales[:], start=True, stop=True)
         exp_score = sb.tile([ROWS, SLOTS], F32)
         nc.scalar.activation(out=exp_score[:], in_=score[:], func=ACT.Exp)
-        gout_bf = interleave("gout_bf", gout_raw, "key_words")
+        gout_bf = sb.tile([P, ROWS, PACK], BF16, tag="key_words", align_bytes=64)
+        interleave(gout_bf, gout_raw)
 
-        val_scales = sb.tile([P, SLOTS], U8, tag="key_pool", align_bytes=64)
+        val_scales = turns.tile([P, SLOTS], U8, offset=0, align_bytes=64)
         nc.vector.tensor_copy(val_scales[:], val_scale_pool[:].indirect(slot_list[:]))
+        val_words = [sb.tile([P, HALF], U32, name="val_words_low", align_bytes=64),
+                     sb.tile([P, HALF], U32, name="val_words_high", tag="pquery_raw", align_bytes=64)]
+        nc.vector.tensor_copy(val_words[0][:], val_pool[:].indirect(slot_list[:, : HALF // 16]))
 
-        gated = sb.tile([ROWS, SLOTS], F32, tag="val_scale_pool", align_bytes=64)
+        gated = turns.tile([ROWS, SLOTS], F32, offset=4 * POOL, align_bytes=64)
         gated_sum = sb.tile([ROWS, 1], F32)
         nc.vector.scalar_tensor_tensor(
             out=gated[:].rearrange("q (g i) -> q g i", i=PER_PAGE),
             in0=half_tanh[:].unsqueeze(2).to_broadcast([ROWS, PAGES, PER_PAGE]), scalar=1.0,
             in1=exp_score[:].rearrange("q (g i) -> q g i", i=PER_PAGE),
             op0=ALU.add, op1=ALU.mult, accum_out=gated_sum[:])
-        gout_codes, gout_scales = quantize("gout", gout_bf, ROWS, "half_tanh")
-        total = sb.tile([ROWS, 1], F32, tag="pquery_raw", align_bytes=64)
-        nc.scalar.activation(out=total[:], in_=reserve_sb[:], func=ACT.Identity, scale=2.0, bias=gated_sum[:])
+        gout_codes, gout_scales = quantize("gout", gout_bf, ROWS, "gout_codes")
+        nc.vector.tensor_copy(val_words[1][:], val_pool[:].indirect(slot_list[:, HALF // 16 :]))
+        total = sb.tile([ROWS, 1], F32)
+        nc.scalar.activation(out=total[:], in_=gated_sum[:], func=ACT.Identity, bias=twice_reserve[:])
 
-        val_words = sb.tile([P, SLOTS], U32, tag="key_words", align_bytes=64)
         dread = ps.tile([ROWS, SLOTS], F32)
         for h in range(2):
             cols = slice(h * HALF, (h + 1) * HALF)
-            nc.vector.tensor_copy(val_words[:, cols],
-                                  val_pool[:].indirect(slot_list[:, h * HALF // 16 : (h + 1) * HALF // 16]))
             nc.tensor.matmul_mx(out=dread[:, cols], lhsT=gout_codes[:].bitcast(FP8X4), lhsT_scale=gout_scales[:],
-                                rhs=val_words[:, cols].bitcast(FP8X4), rhs_scale=val_scales[VALS_PLANE:P, cols],
+                                rhs=val_words[h][:].bitcast(FP8X4), rhs_scale=val_scales[VALS_PLANE:P, cols],
                                 start=True, stop=True)
-        inv_total = sb.tile([ROWS, 1], F32, tag="val_pool", align_bytes=64)
+        inv_total = sb.tile([ROWS, 1], F32, tag="query_raw", align_bytes=64)
         nc.vector.reciprocal(inv_total[:], total[:])
         weight = sb.tile([ROWS, SLOTS], F32)
         nc.scalar.activation(out=weight[:], in_=gated[:], func=ACT.Copy, scale=inv_total[:])

import math
from contextlib import ExitStack

import concourse.mybir as mybir

F32 = mybir.dt.float32
BF16 = mybir.dt.bfloat16
I32 = mybir.dt.int32
U32 = mybir.dt.uint32
U16 = mybir.dt.uint16
U8 = mybir.dt.uint8
FP8X4 = mybir.dt.float8_e4m3fn_x4
ACT = mybir.ActivationFunctionType
ALU = mybir.AluOpType

P = 128
PACK = 4
POOL = 2048
SLOTS = 512
ROWS = 128
PAGES = 64
TABLE = 256
PER_PAGE = SLOTS // PAGES
HALF = SLOTS // 2
VALS_PLANE = 4
PENALTY = 512.0 * 2.0 * 512.0
ROOT = math.sqrt(PENALTY)

FLOPS = 2 * 512 * ROWS * (SLOTS + SLOTS + PAGES)


def tile_attend_gppagetablegate_kernel(tc, query, pquery, keys_words, keys_scales, pgsum, reserve, gout,
                                        vals_words, vals_scales, base, offs2, offs, out):
    nc = tc.nc
    with ExitStack() as ctx:
        sb = ctx.enter_context(tc.tile_pool(name="sb", bufs=1))
        turns = ctx.enter_context(tc.tile_pool(name="turns", bufs=1))
        ps = ctx.enter_context(tc.psum_pool(name="ps", bufs=1))

        def load_words(pool, words):
            nc.sync.dma_start(out=pool[:].bitcast(I32), in_=words[0].rearrange("p n t -> p (n t)").bitcast(I32))

        def load_scales(pool, scales, first):
            for j in range(4):
                nc.sync.dma_start(out=pool[first + j : P : 32, :].bitcast(I32), in_=scales[0, j:16:4, :].bitcast(I32))

        def load_rows(name, src, width, tag):
            raw = sb.tile([P, PACK, width], F32, name=name, tag=tag, align_bytes=64)
            nc.sync.dma_start(out=raw[:], in_=src.rearrange("(p j) w -> p j w", j=PACK))
            return raw

        def interleave(grouped, raw):
            nc.scalar.activation(out=grouped[:].rearrange("p (c i) t -> p c t i", i=4),
                                 in_=raw[:].rearrange("p t (c i) -> p c t i", i=4), func=ACT.Copy)

        def quantize(name, grouped, width, tag):
            codes = sb.tile([P, width], U32, name=name + "_codes", tag=tag, align_bytes=64)
            scales = sb.tile([P, width], U8, name=name + "_scales", align_bytes=64)
            nc.vector.quantize_mx(out=codes[:].bitcast(FP8X4), scales=scales[:],
                                  in_=grouped[:].rearrange("p w j -> p (w j)"))
            return codes, scales

        key_scale_pool = sb.tile([P, POOL], U8, tag="key_scale_pool", align_bytes=64)
        nc.vector.memset(key_scale_pool[:].bitcast(I32), 0)

        reserve_sb = turns.tile([ROWS, 16], F32, offset=4 * POOL - 32)
        nc.sync.dma_start(out=reserve_sb[:, 0:1], in_=reserve)
        page_list = sb.tile([P, PAGES // 16], U16)
        nc.sync.dma_start(page_list[:], offs2)
        slot_list = sb.tile([P, SLOTS // 16], U16)
        nc.sync.dma_start(slot_list[:], offs)
        pgsum_raw = load_rows("pgsum_raw", pgsum, TABLE, "pgsum_raw")
        pquery_raw = load_rows("pquery_raw", pquery, ROWS, "pquery_raw")
        query_raw = load_rows("query_raw", query, ROWS, "query_raw")
        load_scales(key_scale_pool, keys_scales, 0)
        twice_reserve = sb.tile([ROWS, 1], F32)
        nc.vector.tensor_scalar_mul(twice_reserve[:], reserve_sb[:, 0:1], 2.0)
        key_pool = turns.tile([P, POOL], U32, offset=0, align_bytes=64)
        load_words(key_pool, keys_words)
        val_scale_pool = turns.tile([P, POOL], U8, offset=4 * POOL, align_bytes=64)
        nc.vector.memset(val_scale_pool[:].bitcast(I32), 0)
        load_scales(val_scale_pool, vals_scales, VALS_PLANE)

        pages_bf = sb.tile([P, PAGES, PACK], BF16, align_bytes=64)
        for j in range(PACK):
            nc.vector.tensor_copy(pages_bf[:, :, j], pgsum_raw[:, j, :].indirect(page_list[:]))
        pquery_bf = sb.tile([P, ROWS, PACK], BF16, align_bytes=64)
        interleave(pquery_bf, pquery_raw)
        gout_raw = load_rows("gout_raw", gout, ROWS, "pquery_raw")
        query_bf = sb.tile([P, ROWS, PACK], BF16, tag="query_bf", align_bytes=64)
        interleave(query_bf, query_raw)
        val_pool = sb.tile([P, POOL], U32, tag="query_raw", align_bytes=64)
        load_words(val_pool, vals_words)
        key_scales = sb.tile([P, SLOTS], U8, align_bytes=64)
        nc.vector.tensor_copy(key_scales[:], key_scale_pool[:].indirect(slot_list[:]))
        pquery_codes, pquery_scales = quantize("pquery", pquery_bf, ROWS, "pquery_codes")
        page_codes, page_scales = quantize("page", pages_bf, PAGES, "page_codes")
        query_codes, query_scales = quantize("query", query_bf, ROWS, "key_scale_pool")
        base_sb = sb.tile([ROWS, SLOTS], F32, tag="query_bf", align_bytes=64)
        nc.sync.dma_start(out=base_sb[:], in_=base)
        page_score = ps.tile([ROWS, PAGES], F32)
        nc.tensor.matmul_mx(out=page_score[:], lhsT=pquery_codes[:].bitcast(FP8X4), lhsT_scale=pquery_scales[:],
                            rhs=page_codes[:].bitcast(FP8X4), rhs_scale=page_scales[:], start=True, stop=True)
        half_tanh = sb.tile([ROWS, PAGES], F32)
        nc.scalar.activation(out=half_tanh[:], in_=page_score[:], func=ACT.Tanh, scale=0.5)

        key_words = sb.tile([P, SLOTS], U32, tag="key_words", align_bytes=64)
        nc.vector.tensor_copy(key_words[:], key_pool[:].indirect(slot_list[:]))
        score = ps.tile([ROWS, SLOTS], F32)
        nc.tensor.matmul_mx(out=score[:], lhsT=query_codes[:].bitcast(FP8X4), lhsT_scale=query_scales[:],
                            rhs=key_words[:].bitcast(FP8X4), rhs_scale=key_scales[:], start=True, stop=True)
        exp_score = sb.tile([ROWS, SLOTS], F32)
        nc.scalar.activation(out=exp_score[:], in_=score[:], func=ACT.Exp)
        gout_bf = sb.tile([P, ROWS, PACK], BF16, tag="key_words", align_bytes=64)
        interleave(gout_bf, gout_raw)

        val_scales = turns.tile([P, SLOTS], U8, offset=0, align_bytes=64)
        nc.vector.tensor_copy(val_scales[:], val_scale_pool[:].indirect(slot_list[:]))
        val_words = [sb.tile([P, HALF], U32, name="val_words_low", align_bytes=64),
                     sb.tile([P, HALF], U32, name="val_words_high", tag="pquery_raw", align_bytes=64)]
        nc.vector.tensor_copy(val_words[0][:], val_pool[:].indirect(slot_list[:, : HALF // 16]))

        gated = turns.tile([ROWS, SLOTS], F32, offset=4 * POOL, align_bytes=64)
        gated_sum = sb.tile([ROWS, 1], F32)
        nc.vector.scalar_tensor_tensor(
            out=gated[:].rearrange("q (g i) -> q g i", i=PER_PAGE),
            in0=half_tanh[:].unsqueeze(2).to_broadcast([ROWS, PAGES, PER_PAGE]), scalar=1.0,
            in1=exp_score[:].rearrange("q (g i) -> q g i", i=PER_PAGE),
            op0=ALU.add, op1=ALU.mult, accum_out=gated_sum[:])
        gout_codes, gout_scales = quantize("gout", gout_bf, ROWS, "gout_codes")
        nc.vector.tensor_copy(val_words[1][:], val_pool[:].indirect(slot_list[:, HALF // 16 :]))
        total = sb.tile([ROWS, 1], F32)
        nc.scalar.activation(out=total[:], in_=gated_sum[:], func=ACT.Identity, bias=twice_reserve[:])

        dread = ps.tile([ROWS, SLOTS], F32)
        for h in range(2):
            cols = slice(h * HALF, (h + 1) * HALF)
            nc.tensor.matmul_mx(out=dread[:, cols], lhsT=gout_codes[:].bitcast(FP8X4), lhsT_scale=gout_scales[:],
                                rhs=val_words[h][:].bitcast(FP8X4), rhs_scale=val_scales[VALS_PLANE:P, cols],
                                start=True, stop=True)
        inv_total = sb.tile([ROWS, 1], F32, tag="query_raw", align_bytes=64)
        nc.vector.reciprocal(inv_total[:], total[:])
        weight = sb.tile([ROWS, SLOTS], F32)
        nc.scalar.activation(out=weight[:], in_=gated[:], func=ACT.Copy, scale=inv_total[:])
        weight_sq = sb.tile([ROWS, SLOTS], F32)
        nc.scalar.activation(out=weight_sq[:], in_=weight[:], func=ACT.Square, scale=math.sqrt(ROOT / 2.0))

        scratch_v = sb.tile([ROWS, SLOTS], F32)
        mean = sb.tile([ROWS, 1], F32)
        nc.vector.scalar_tensor_tensor(out=scratch_v[:], in0=dread[:], scalar=inv_total[:], in1=gated[:],
                                       op0=ALU.mult, op1=ALU.mult, accum_out=mean[:])
        dscore = sb.tile([ROWS, SLOTS], F32)
        nc.vector.scalar_tensor_tensor(out=dscore[:], in0=dread[:], scalar=mean[:], in1=weight[:],
                                       op0=ALU.subtract, op1=ALU.mult)
        shift = sb.tile([ROWS, 1], F32)
        nc.vector.scalar_tensor_tensor(out=scratch_v[:], in0=dread[:], scalar=mean[:], in1=weight_sq[:],
                                       op0=ALU.subtract, op1=ALU.mult, accum_out=shift[:])
        scratch_s = sb.tile([ROWS, SLOTS], F32)
        energy = sb.tile([ROWS, 1], F32)
        nc.scalar.activation(out=scratch_s[:], in_=dscore[:], func=ACT.Square, scale=ROOT, accum_out=energy[:])
        shift_sq = sb.tile([ROWS, 1], F32)
        nc.scalar.activation(out=shift_sq[:], in_=shift[:], func=ACT.Square)

        squares = []
        rests = []
        for h in range(2):
            cols = slice(h * HALF, (h + 1) * HALF)
            square = sb.tile([ROWS, HALF], F32, name="square%d" % h)
            nc.scalar.activation(out=square[:], in_=dscore[:, cols], func=ACT.Square, scale=-ROOT, bias=shift[:])
            rest = sb.tile([ROWS, HALF], F32, name="rest%d" % h)
            nc.vector.scalar_tensor_tensor(out=rest[:], in0=weight[:, cols], scalar=energy[:], in1=base_sb[:, cols],
                                           op0=ALU.mult, op1=ALU.subtract)
            squares.append(square)
            rests.append(rest)
        for h in range(2):
            cols = slice(h * HALF, (h + 1) * HALF)
            result = sb.tile([ROWS, HALF], F32, name="result%d" % h)
            nc.vector.scalar_tensor_tensor(out=result[:], in0=squares[h][:], scalar=shift_sq[:], in1=rests[h][:],
                                           op0=ALU.subtract, op1=ALU.subtract)
            nc.sync.dma_start(out=out[:, cols], in_=result[:])
